import numpy as np
import ml_dtypes


def mxq(x, axis, fmt="e4m3"):
    dtype, down = {"e4m3": (ml_dtypes.float8_e4m3fn, 7), "e5m2": (ml_dtypes.float8_e5m2, 14)}[fmt]
    v = np.moveaxis(np.asarray(x, np.float32).astype(ml_dtypes.bfloat16).astype(np.float64), axis, -1)
    blocks = v.reshape(v.shape[:-1] + (-1, 32))
    amax = np.abs(blocks).max(-1, keepdims=True)
    byte = np.maximum(np.where(amax > 0, np.frexp(amax)[1] - 1 + 127, 0) - down, 1)
    scale = np.exp2(byte - 127.0)
    codes = (blocks / scale).astype(np.float32).astype(dtype).astype(np.float64)
    return np.moveaxis((codes * scale).reshape(v.shape), -1, axis)


WIDE = False


def mx_kscale(k):
    if not WIDE:
        return np.ones(k)
    levels = np.array([10, -10, 5, -5, 0])
    if k % 512:
        return np.exp2(np.random.permutation(np.resize(levels, k // 32))).repeat(32)
    a = np.empty((k // 512, 16))
    for p in range(k // 512):
        a[p, :8] = np.random.permutation(np.resize(levels, 8))
        for g in range(8):
            far = levels[np.abs(levels - a[p, g]) >= 10]
            a[p, g + 8] = far[np.random.randint(len(far))]
    return np.exp2(a.ravel()).repeat(32)


def f64(x):
    return np.asarray(x).astype(np.float64)


def striped(idx):
    return np.tile(idx.reshape(-1, 16).T, (8, 1)).astype(np.uint16)


def unstriped(offs):
    return offs[:16].T.reshape(-1).astype(np.int64)


E2M1 = np.array([0.0, 0.5, 1.0, 1.5, 2.0, 3.0, 4.0, 6.0, -0.0, -0.5, -1.0, -1.5, -2.0, -3.0, -4.0, -6.0])


def pack_weight(w, fmt):
    k, n = w.shape
    w = f64(np.asarray(w, np.float32).astype(ml_dtypes.bfloat16)).reshape(k // 32, 32, n)
    amax = np.abs(w).max(1)
    if fmt == "e4m3":
        byte = np.frexp(amax)[1] - 1 + 127 - 7
    else:
        mant, ex = np.frexp(amax / 6.0)
        byte = np.where(mant > 0.5, ex, ex - 1) + 127
    byte = np.clip(np.where(amax > 0, byte, 1), 1, 254)
    scaled = (w * np.exp2(127.0 - byte)[:, None, :]).reshape(k, n).astype(np.float32)
    by_word = np.ascontiguousarray(scaled.reshape(k // 512, 128, 4, n).transpose(0, 1, 3, 2))
    if fmt == "e4m3":
        words = by_word.astype(ml_dtypes.float8_e4m3fn).view(np.uint8)
    else:
        c = by_word.astype(ml_dtypes.float4_e2m1fn).view(np.uint8) & 0xF
        words = (c[..., 0::2] | (c[..., 1::2] << 4)).reshape(k // 512, 128, 2 * n)
    return np.ascontiguousarray(words), np.ascontiguousarray(byte.astype(np.uint8).reshape(k // 512, 16, n))


def unpack_weight(words, scales, fmt):
    g, _, n = scales.shape
    words = np.ascontiguousarray(words).reshape(g, 128, n, -1)
    if fmt == "e4m3":
        vals = words.view(ml_dtypes.float8_e4m3fn).astype(np.float64)
    else:
        nib = np.empty((g, 128, n, 4), np.uint8)
        nib[..., 0::2] = words & 0xF
        nib[..., 1::2] = words >> 4
        vals = E2M1[nib]
    vals = vals * np.repeat(np.exp2(scales.astype(np.float64) - 127.0), 8, axis=1)[..., None]
    return vals.transpose(0, 1, 3, 2).reshape(g * 512, n)


def gelu(v):
    return 0.5 * v * (1.0 + np.tanh(np.sqrt(2.0 / np.pi) * (v + 0.044715 * v**3)))


K, H, T, S, T2, P = 1024, 1024, 2048, 512, 1024, 512

def setup_inputs():
    n = np.random.standard_normal
    s = mx_kscale(K)[:, None]
    u = mx_kscale(H)[:, None]
    tab_words, tab_scales = pack_weight(n((K, T)) * s, "e4m3")
    w2_words, w2_scales = pack_weight(1.3 * n((K, H)) / np.sqrt(K) / s, "e2m1")
    sign = np.where(n(H) > 0, 1.0, -1.0)
    return {
        "tab_words": tab_words, "tab_scales": tab_scales,
        "offs": striped(np.random.permutation(T)[:S]),
        "offs2": striped(np.random.permutation(T2)[:S]),
        "offs3": striped(np.random.permutation(T2)[:P]),
        "offs4": striped(np.random.permutation(T2)[:P]),
        "w1": (0.4 * n((K, H)) / np.sqrt(K) / s).astype(np.float32),
        "w2_words": w2_words, "w2_scales": w2_scales,
        "w3": (0.52 * n((K, H)) / np.sqrt(K) / s).astype(np.float32),
        "gain": (1.5 * np.exp(0.3 * n(H)) * u[:, 0]).astype(np.float32),
        "wgs": np.exp(0.3 * n((128, S))).astype(np.float32),
        "page0": (n((H, T2)) * u).astype(np.float32),
        "shift": (0.8 * n(H) * u[:, 0]).astype(np.float32),
        "mvec": (0.5 * sign * np.random.uniform(0.6, 1.4, H) / np.sqrt(H) / u[:, 0] ** 2).astype(np.float32),
        "pad": np.exp(0.4 * n(P)).astype(np.float32),
    }

def reference(tab_words, tab_scales, offs, offs2, offs3, offs4, w1, w2_words, w2_scales, w3, gain, wgs, page0, shift, mvec, pad):
    v = unpack_weight(tab_words, tab_scales, "e4m3")[:, unstriped(offs)]
    w2 = unpack_weight(w2_words, w2_scales, "e2m1")
    base = mxq(f64(w1), 0, "e4m3").T @ v
    bend = np.tanh(w2.T @ v)
    wave = np.sin(mxq(f64(w3), 0, "e4m3").T @ v)
    h = (base + bend + wave) * f64(gain)[:, None]
    page = f64(page0).copy()
    page[:, unstriped(offs2)] = np.tile(f64(wgs), (H // 128, 1)) * h
    x1 = page[:, unstriped(offs3)]
    x2 = (page[:, unstriped(offs4)] + f64(shift)[:, None]) * f64(mvec)[:, None]
    e = mxq(x1, 0, "e4m3").T @ mxq(x2, 0, "e4m3")
    return e * f64(pad)[None, :]

@@ -1,0 +1,364 @@
+import math
+from contextlib import ExitStack
+
+import concourse.mybir as mybir
+from concourse.masks import make_identity
+
+K, H, T, S, T2, NP = 1024, 1024, 2048, 512, 1024, 512
+FLOPS = 2 * 3 * K * H * S + 2 * H * NP * NP
+
+F32 = mybir.dt.float32
+BF16 = mybir.dt.bfloat16
+I32 = mybir.dt.int32
+U32 = mybir.dt.uint32
+U16 = mybir.dt.uint16
+U8 = mybir.dt.uint8
+FP8X4 = mybir.dt.float8_e4m3fn_x4
+FP4X4 = mybir.dt.float4_e2m1fn_x4
+ACT = mybir.ActivationFunctionType
+ALU = mybir.AluOpType
+
+P = 128
+PACK = 4
+PASS = P * PACK
+PASSES = K // PASS
+HALVES = H // PASS
+SLICES = HALVES * PACK
+BLOCKS = S // P
+QUADS = 4
+
+
+def tile_list_slurry_pad_match_kernel(
+    tc, tab_words, tab_scales, offs, offs2, offs3, offs4, w1, w2_words, w2_scales, w3, gain, wgs, page0, shift, mvec, pad, out
+):
+    nc = tc.nc
+    with ExitStack() as ctx:
+        lists = ctx.enter_context(tc.tile_pool(name="lists", bufs=1))
+        keep = ctx.enter_context(tc.tile_pool(name="keep", bufs=1))
+        ring = ctx.enter_context(tc.tile_pool(name="ring", bufs=2))
+        psum = ctx.enter_context(tc.psum_pool(name="psum", bufs=2))
+
+        def load_list(src, name):
+            tile = lists.tile([P, S // 16], U16, name=name)
+            nc.sync.dma_start(tile[:], src)
+            return tile
+
+        def load_scale_rows(tile, src):
+            for q in range(QUADS):
+                nc.sync.dma_start(
+                    tile[32 * q : 32 * q + 4, :, :].bitcast(I32),
+                    src[:, 4 * q : 4 * q + 4, :].rearrange("a r c -> r a c").bitcast(I32),
+                )
+
+        def load_row_vector(src, name):
+            tile = keep.tile([P, HALVES, PACK], F32, name=name)
+            nc.gpsimd.dma_start(tile[:], src.rearrange("(b p t) -> p b t", p=P, t=PACK))
+            return tile
+
+        raw = {}
+
+        def load_weight(name, w, b, a):
+            tile = ring.tile([P, PACK, PASS], F32, name="raw", tag="raw", bufs=5)
+            rows = w[a * PASS : (a + 1) * PASS, b * PASS : (b + 1) * PASS]
+            nc.sync.dma_start(tile[:], rows.rearrange("(p i) c -> p i c", i=PACK))
+            raw[name, b, a] = tile
+
+        pages = {}
+
+        def load_page(s):
+            b, t = divmod(s, PACK)
+            tile = ring.tile([P, T2], F32, name="page", tag="page", bufs=6)
+            rows = page0[b * PASS : (b + 1) * PASS, :].rearrange("(p t) c -> p t c", t=PACK)
+            nc.sync.dma_start(tile[:], rows[:, t, :])
+            pages[s] = tile
+
+        tab_scale_rows = keep.tile([P, PASSES, T], U8, name="tab_scale_rows", align_bytes=64)
+        nc.vector.memset(tab_scale_rows[:].bitcast(I32), 0)
+        w2_scale_rows = keep.tile([P, PASSES, H], U8, name="w2_scale_rows", align_bytes=64)
+        nc.vector.memset(w2_scale_rows[:].bitcast(I32), 0)
+        ident = keep.tile([P, P], F32, name="ident")
+        make_identity(nc, ident[:])
+        gains = load_row_vector(gain, "gains")
+        shifts = load_row_vector(shift, "shifts")
+        mvecs = load_row_vector(mvec, "mvecs")
+
+        table = []
+
+        def load_table(a):
+            tile = keep.tile([P, T], U32, name="table%d" % a, align_bytes=64)
+            nc.sync.dma_start(tile[:].bitcast(I32), tab_words[a].rearrange("p t i -> p (t i)").bitcast(I32))
+            table.append(tile)
+
+        wgs_rows = {}
+
+        def load_wgs(first, count):
+            tile = keep.tile([P, count, S], F32, name="wgs_rows%d" % first)
+            rows = wgs.rearrange("(p t) j -> p t j", t=PACK)[:, first : first + count, :]
+            for q in (0, 2, 1, 3):
+                nc.sync.dma_start(tile[32 * q : 32 * q + 32, :, :], rows)
+            for t in range(count):
+                wgs_rows[first + t] = tile[:, t, :]
+
+        pick = load_list(offs, "pick")
+        load_table(0)
+        place = load_list(offs2, "place")
+        pick_pad = load_list(offs4, "pick_pad")
+        load_scale_rows(tab_scale_rows, tab_scales)
+        load_table(1)
+        w2_codes = keep.tile([P, PASSES, 2 * H], U8, name="w2_codes", align_bytes=64)
+        nc.sync.dma_start(w2_codes[:].bitcast(I32), w2_words.rearrange("a p c -> p a c").bitcast(I32))
+        load_scale_rows(w2_scale_rows, w2_scales)
+        load_weight("w3", w3, 0, 0)
+        load_weight("w3", w3, 0, 1)
+        load_weight("w1", w1, 0, 0)
+        load_weight("w1", w1, 0, 1)
+        load_wgs(0, 1)
+        load_page(0)
+        pick_slurry = load_list(offs3, "pick_slurry")
+        load_wgs(1, PACK - 1)
+        load_page(1)
+        load_weight("w3", w3, 1, 0)
+        load_weight("w3", w3, 1, 1)
+        load_weight("w1", w1, 1, 0)
+        load_weight("w1", w1, 1, 1)
+        for s in range(2, 6):
+            load_page(s)
+        pad_rows = keep.tile([P, NP], F32, name="pad_rows")
+        nc.sync.dma_start(pad_rows[:], pad.partition_broadcast(P))
+
+        v_codes, v_scales = [], []
+        for a in range(PASSES):
+            scales = keep.tile([P, S], U8, name="v_scales%d" % a, align_bytes=64)
+            nc.vector.tensor_copy(scales[:], tab_scale_rows[:, a, :].indirect(pick[:]))
+            codes = keep.tile([P, S], U32, name="v_codes%d" % a, align_bytes=64)
+            nc.vector.tensor_copy(codes[:], table[a][:].indirect(pick[:]))
+            v_codes.append(codes)
+            v_scales.append(scales)
+
+        w_codes, w_scales = {}, {}
+
+        def cast(engine, dst, src):
+            if engine == "vector":
+                nc.vector.tensor_copy(dst, src)
+            elif engine == "scalar":
+                nc.scalar.copy(dst, src)
+            else:
+                nc.gpsimd.tensor_scalar(dst, src, 1.0, 0.0, ALU.mult, ALU.add)
+
+        def quantise_weight(name, b, a, pair, engine, tag="grouped", bufs=4):
+            grouped = ring.tile([P, 2, P, PACK], BF16, name="grouped", tag=tag, bufs=bufs, align_bytes=64)
+            src = raw[name, b, a][:].rearrange("p i (m t) -> p m i t", t=PACK)[:, :, :, 2 * pair : 2 * pair + 2]
+            cast(engine, grouped[:].rearrange("p t m i -> p m i t"), src)
+            label = "%s_%d%d%d" % (name, b, a, pair)
+            codes = keep.tile([P, 2 * P], U32, name="c" + label, align_bytes=64)
+            scales = keep.tile([P, 2 * P], U8, name="s" + label, align_bytes=64)
+            nc.vector.quantize_mx(out=codes[:].bitcast(FP8X4), scales=scales[:], in_=grouped[:].rearrange("p t m i -> p (t m i)"))
+            w_codes[name, b, a, pair] = codes
+            w_scales[name, b, a, pair] = scales
+
+        def product(name, s, tag):
+            b, t = divmod(s, PACK)
+            pair, cols = t // 2, slice((t % 2) * P, (t % 2 + 1) * P)
+            acc = psum.tile([P, BLOCKS, P], F32, name=tag, tag=tag, bufs=1)
+            for jb in range(BLOCKS):
+                picked = slice(jb * P, (jb + 1) * P)
+                for a in range(PASSES):
+                    nc.tensor.matmul_mx(
+                        out=acc[:, jb, :],
+                        lhsT=v_codes[a][:, picked].bitcast(FP8X4),
+                        lhsT_scale=v_scales[a][:, picked],
+                        rhs=w_codes[name, b, a, pair][:, cols].bitcast(FP8X4),
+                        rhs_scale=w_scales[name, b, a, pair][:, cols],
+                        start=(a == 0),
+                        stop=(a == PASSES - 1),
+                    )
+            return acc
+
+        def add_transposed(acc, terms):
+            for n, term in enumerate(terms):
+                for jb in range(BLOCKS):
+                    nc.tensor.matmul(
+                        acc[:, jb, :], term[:, jb, :], ident[:], is_transpose=True,
+                        start=(n == 0 and jb == 0), stop=(n == len(terms) - 1 and jb == BLOCKS - 1),
+                    )
+
+        bend = {}
+
+        def make_bend(b):
+            tile = ring.tile([P, BLOCKS, PACK, P], F32, name="bend", tag="bend")
+            for jb in range(BLOCKS):
+                picked = slice(jb * P, (jb + 1) * P)
+                acc = psum.tile([P, PASS], F32, name="acc_bend", tag="acc_sum")
+                for a in range(PASSES):
+                    nc.tensor.matmul_mx(
+                        out=acc[:],
+                        lhsT=v_codes[a][:, picked].bitcast(FP8X4),
+                        lhsT_scale=v_scales[a][:, picked],
+                        rhs=w2_codes[:, a, 2 * b * PASS : 2 * (b + 1) * PASS].bitcast(FP4X4),
+                        rhs_scale=w2_scale_rows[:, a, b * PASS : (b + 1) * PASS],
+                        start=(a == 0),
+                        stop=(a == PASSES - 1),
+                    )
+                nc.scalar.activation(tile[:, jb, :, :], acc[:].rearrange("p (m t) -> p t m", t=PACK), ACT.Tanh)
+            bend[b] = tile
+
+        reduced, wave, base, feat = {}, {}, {}, {}
+
+        def wave_on_vector(s):
+            acc = product("w3", s, "acc_first")[:].rearrange("p b m -> p (b m)")
+            count = ring.tile([P, S], I32, name="count", tag="turns")
+            nc.vector.tensor_scalar(count[:], acc, 1 / (2 * math.pi), None, ALU.mult)
+            rest = ring.tile([P, S], F32, name="rest", tag="reduced")
+            nc.vector.scalar_tensor_tensor(rest[:], count[:], -2 * math.pi, acc, ALU.mult, ALU.add)
+            wave[s] = ring.tile([P, BLOCKS, P], F32, name="wave", tag="wave", bufs=1, align_bytes=64)
+            nc.scalar.activation(wave[s][:].rearrange("p b m -> p (b m)"), rest[:], ACT.Sin)
+
+        def wave_front(s, tag="acc_w"):
+            acc = product("w3", s, tag)
+            folded = ring.tile([P, S], F32, name="folded", tag="folded")
+            nc.scalar.activation(folded[:], acc[:].rearrange("p b m -> p (b m)"), ACT.Abs, bias=-math.pi / 2)
+            turns = ring.tile([P, S], U32, name="turns", tag="turns")
+            nc.scalar.activation(turns[:], folded[:], ACT.Copy, scale=1 / (2 * math.pi), bias=0.25)
+            reduced[s] = ring.tile([P, S], F32, name="reduced", tag="reduced")
+            nc.vector.scalar_tensor_tensor(reduced[s][:], turns[:].bitcast(I32), -2 * math.pi, folded[:], ALU.mult, ALU.add)
+
+        def wave_back(s):
+            wave[s] = ring.tile([P, BLOCKS, P], F32, name="wave", tag="wave", bufs=1, align_bytes=64)
+            nc.scalar.activation(wave[s][:].rearrange("p b m -> p (b m)"), reduced[s][:], ACT.Sin, bias=math.pi / 2)
+
+        def make_base(s):
+            acc = product("w1", s, "acc_w")
+            base[s] = ring.tile([P, BLOCKS, P], F32, name="base", tag="base")
+            nc.scalar.copy(base[s][:], acc[:])
+
+        def make_feat(s):
+            b, t = divmod(s, PACK)
+            acc = psum.tile([P, BLOCKS, P], F32, name="acc_sum", tag="acc_sum")
+            add_transposed(acc, [wave[s][:], bend[b][:, :, t, :], base[s][:]] if s == 0 else [base[s][:], bend[b][:, :, t, :], wave[s][:]])
+            feat[s] = ring.tile([P, S], F32, name="feat", tag="feat")
+            nc.scalar.activation(feat[s][:], acc[:].rearrange("p b m -> p (b m)"), ACT.Copy, scale=gains[:, b, t : t + 1])
+
+        slots = {}
+        for b in range(HALVES):
+            for side in ("x1", "x2"):
+                slots[side, b] = keep.tile([P, PACK, NP], BF16, name="slots_%s%d" % (side, b))
+        fetched = {}
+
+        def put(s):
+            nc.vector.tensor_tensor(pages[s][:].indirect(place[:]), feat[s][:], wgs_rows[s % PACK], ALU.mult)
+
+        def fetch(s):
+            b, t = divmod(s, PACK)
+            fetched[s] = ring.tile([P, NP], F32, name="fetched", tag="fetched")
+            nc.vector.tensor_copy(fetched[s][:], pages[s][:].indirect(pick_pad[:]))
+            nc.vector.tensor_copy(slots["x1", b][:, t, :], pages[s][:].indirect(pick_slurry[:]))
+
+        shift_mvec = keep.tile([P, 1], F32, name="shift_mvec")
+        nc.gpsimd.tensor_tensor(shift_mvec[:], shifts[:, HALVES - 1, PACK - 1 :], mvecs[:, HALVES - 1, PACK - 1 :], ALU.mult)
+
+        def pad_side(s):
+            b, t = divmod(s, PACK)
+            nc.gpsimd.tensor_scalar(
+                slots["x2", b][:, t, :], fetched[s][:], shifts[:, b, t : t + 1], mvecs[:, b, t : t + 1], ALU.add, ALU.mult
+            )
+
+        woven, x_codes, x_scales = {}, {}, {}
+
+        def open_side(side, b, tag):
+            woven[side, b] = ring.tile([P, NP, PACK], BF16, name="woven", tag=tag, bufs=1, align_bytes=64)
+            x_codes[side, b] = keep.tile([P, NP], U32, name="c%s%d" % (side, b), align_bytes=64)
+            x_scales[side, b] = keep.tile([P, NP], U8, name="s%s%d" % (side, b), align_bytes=64)
+
+        def weave(side, b, half, engine):
+            if half == 0:
+                open_side(side, b, "woven" + side)
+            cols = slice(half * NP // 2, (half + 1) * NP // 2)
+            dst = woven[side, b][:, cols, :].rearrange("p (c i) t -> p c t i", i=4)
+            src = slots[side, b][:, :, cols].rearrange("p t (c i) -> p c t i", i=4)
+            cast(engine, dst, src)
+
+        def quantise_x(side, b, half):
+            cols = slice(half * NP // 2, (half + 1) * NP // 2)
+            nc.vector.quantize_mx(
+                out=x_codes[side, b][:, cols].bitcast(FP8X4),
+                scales=x_scales[side, b][:, cols],
+                in_=woven[side, b][:, cols, :].rearrange("p c t -> p (c t)"),
+            )
+
+        def weave_and_quantise(side, b, half):
+            weave(side, b, half, "scalar")
+            quantise_x(side, b, half)
+
+        make_bend(0)
+        make_bend(1)
+        quantise_weight("w3", 0, 0, 0, "vector")
+        quantise_weight("w3", 0, 1, 0, "vector")
+        wave_on_vector(0)
+        quantise_weight("w1", 0, 0, 0, "scalar")
+        quantise_weight("w1", 0, 1, 0, "vector", "in_turn", 1)
+        make_base(0)
+        make_feat(0)
+        wave_front(1, "acc_first")
+        quantise_weight("w3", 0, 0, 1, "vector")
+        quantise_weight("w3", 0, 1, 1, "vector")
+        wave_front(2)
+        quantise_weight("w1", 0, 0, 1, "vector", "in_turn", 1)
+        quantise_weight("w1", 0, 1, 1, "vector", "in_turn", 1)
+
+        later = [(quantise_weight, name, 1, a, pair, "scalar") for pair in range(2) for name in ("w3", "w1") for a in range(PASSES)]
+        later += [(weave_and_quantise, side, 0, half) for side in ("x1", "x2") for half in range(2)]
+
+        def fill():
+            if later:
+                step = later.pop(0)
+                step[0](*step[1:])
+
+        for s in range(SLICES):
+            put(s)
+            fetch(s)
+            if s + 6 < SLICES:
+                load_page(s + 6)
+            if s + 1 < SLICES:
+                wave_back(s + 1)
+                make_base(s + 1)
+                fill()
+                make_feat(s + 1)
+            fill()
+            if s + 3 < SLICES:
+                wave_front(s + 3)
+            if s + 1 < SLICES:
+                pad_side(s)
+
+        last = HALVES - 1
+        open_side("x2", last, "wave")
+        early = PACK - 1
+        nc.scalar.copy(woven["x2", last][:, :, :early], slots["x2", last][:, :early, :].rearrange("p t c -> p c t"))
+        nc.scalar.activation(
+            woven["x2", last][:, :, early], fetched[SLICES - 1][:], ACT.Identity,
+            scale=mvecs[:, last, early:], bias=shift_mvec[:],
+        )
+        weave("x1", last, 0, "vector")
+        weave("x1", last, 1, "scalar")
+        nc.vector.quantize_mx(
+            out=x_codes["x2", last][:].bitcast(FP8X4),
+            scales=x_scales["x2", last][:],
+            in_=woven["x2", last][:].rearrange("p c t -> p (c t)"),
+        )
+        quantise_x("x1", last, 0)
+        quantise_x("x1", last, 1)
+        for mb in range(BLOCKS):
+            acc = psum.tile([P, NP], F32, name="acc_e", tag="acc_e", bufs=BLOCKS)
+            rows = slice(mb * P, (mb + 1) * P)
+            for b in reversed(range(HALVES)):
+                nc.tensor.matmul_mx(
+                    out=acc[:],
+                    lhsT=x_codes["x1", b][:, rows].bitcast(FP8X4),
+                    lhsT_scale=x_scales["x1", b][:, rows],
+                    rhs=x_codes["x2", b][:].bitcast(FP8X4),
+                    rhs_scale=x_scales["x2", b][:],
+                    start=(b == last),
+                    stop=(b == 0),
+                )
+            result = keep.tile([P, NP], F32, name="result%d" % mb)
+            nc.vector.tensor_tensor(result[:], acc[:], pad_rows[:], ALU.mult)
+            nc.sync.dma_start(out[mb * P : (mb + 1) * P, :], result[:])

@@ -58,7 +58,7 @@ def tile_list_slurry_pad_match_kernel(
         raw = {}
 
         def load_weight(name, w, b, a):
-            tile = ring.tile([P, PACK, PASS], F32, name="raw", tag="raw", bufs=5)
+            tile = ring.tile([P, PACK, PASS], F32, name="raw", tag="raw", bufs=4)
             rows = w[a * PASS : (a + 1) * PASS, b * PASS : (b + 1) * PASS]
             nc.sync.dma_start(tile[:], rows.rearrange("(p i) c -> p i c", i=PACK))
             raw[name, b, a] = tile
@@ -67,7 +67,7 @@ def tile_list_slurry_pad_match_kernel(
 
         def load_page(s):
             b, t = divmod(s, PACK)
-            tile = ring.tile([P, T2], F32, name="page", tag="page", bufs=6)
+            tile = ring.tile([P, T2], F32, name="page", tag="page", bufs=5)
             rows = page0[b * PASS : (b + 1) * PASS, :].rearrange("(p t) c -> p t c", t=PACK)
             nc.sync.dma_start(tile[:], rows[:, t, :])
             pages[s] = tile
@@ -78,7 +78,14 @@ def tile_list_slurry_pad_match_kernel(
         nc.vector.memset(w2_scale_rows[:].bitcast(I32), 0)
         ident = keep.tile([P, P], F32, name="ident")
         make_identity(nc, ident[:])
+        unread = keep.tile([P, 1], F32, name="unread")
+        nc.scalar.activation(unread[:], ident[:, 0:1], ACT.Silu)
         gains = load_row_vector(gain, "gains")
+        gain_of = []
+        for s in range(SLICES):
+            column = ring.tile([P, 1], F32, name="gain_column", tag="turn%d" % s, bufs=1, align_bytes=64)
+            nc.gpsimd.tensor_copy(column[:], gains[:, s // PACK, s % PACK : s % PACK + 1])
+            gain_of.append(column)
         shifts = load_row_vector(shift, "shifts")
         mvecs = load_row_vector(mvec, "mvecs")
 
@@ -121,7 +128,7 @@ def tile_list_slurry_pad_match_kernel(
         load_weight("w3", w3, 1, 1)
         load_weight("w1", w1, 1, 0)
         load_weight("w1", w1, 1, 1)
-        for s in range(2, 6):
+        for s in range(2, 5):
             load_page(s)
         pad_rows = keep.tile([P, NP], F32, name="pad_rows")
         nc.sync.dma_start(pad_rows[:], pad.partition_broadcast(P))
@@ -145,8 +152,8 @@ def tile_list_slurry_pad_match_kernel(
             else:
                 nc.gpsimd.tensor_scalar(dst, src, 1.0, 0.0, ALU.mult, ALU.add)
 
-        def quantise_weight(name, b, a, pair, engine, tag="grouped", bufs=4):
-            grouped = ring.tile([P, 2, P, PACK], BF16, name="grouped", tag=tag, bufs=bufs, align_bytes=64)
+        def quantise_weight(name, b, a, pair, engine):
+            grouped = ring.tile([P, 2, P, PACK], BF16, name="grouped", tag="grouped", bufs=3, align_bytes=64)
             src = raw[name, b, a][:].rearrange("p i (m t) -> p m i t", t=PACK)[:, :, :, 2 * pair : 2 * pair + 2]
             cast(engine, grouped[:].rearrange("p t m i -> p m i t"), src)
             label = "%s_%d%d%d" % (name, b, a, pair)
@@ -156,7 +163,28 @@ def tile_list_slurry_pad_match_kernel(
             w_codes[name, b, a, pair] = codes
             w_scales[name, b, a, pair] = scales
 
-        def product(name, s, tag):
+        both = {}
+
+        def round_half(name, b, a, pair, tag="both", bufs=2):
+            if a == 0:
+                both[name, b, pair] = ring.tile([P, PASSES, 2, P, PACK], BF16, name="both", tag=tag, bufs=bufs, align_bytes=64)
+            grouped = both[name, b, pair]
+            src = raw[name, b, a][:].rearrange("p i (m t) -> p m i t", t=PACK)[:, :, :, 2 * pair : 2 * pair + 2]
+            nc.scalar.copy(grouped[:, a].rearrange("p t m i -> p m i t"), src)
+            if a == PASSES - 1:
+                label = "%s_%d%d" % (name, b, pair)
+                codes = keep.tile([P, PASSES, 2 * P], U32, name="c" + label, align_bytes=64)
+                scales = keep.tile([P, PASSES, 2 * P], U8, name="s" + label, align_bytes=64)
+                nc.vector.quantize_mx(
+                    out=codes[:].rearrange("p a c -> p (a c)").bitcast(FP8X4),
+                    scales=scales[:].rearrange("p a c -> p (a c)"),
+                    in_=grouped[:].rearrange("p a t m i -> p (a t m i)"),
+                )
+                for n in range(PASSES):
+                    w_codes[name, b, n, pair] = codes[:, n, :]
+                    w_scales[name, b, n, pair] = scales[:, n, :]
+
+        def product(name, s, tag="acc_w"):
             b, t = divmod(s, PACK)
             pair, cols = t // 2, slice((t % 2) * P, (t % 2 + 1) * P)
             acc = psum.tile([P, BLOCKS, P], F32, name=tag, tag=tag, bufs=1)
@@ -185,10 +213,10 @@ def tile_list_slurry_pad_match_kernel(
         bend = {}
 
         def make_bend(b):
-            tile = ring.tile([P, BLOCKS, PACK, P], F32, name="bend", tag="bend")
+            tile = ring.tile([P, BLOCKS, PACK, P], F32, name="bend", tag="bend%d" % b, bufs=1)
             for jb in range(BLOCKS):
                 picked = slice(jb * P, (jb + 1) * P)
-                acc = psum.tile([P, PASS], F32, name="acc_bend", tag="acc_sum")
+                acc = psum.tile([P, PASS], F32, name="acc_bend", tag="acc_e", bufs=BLOCKS)
                 for a in range(PASSES):
                     nc.tensor.matmul_mx(
                         out=acc[:],
@@ -204,14 +232,12 @@ def tile_list_slurry_pad_match_kernel(
 
         reduced, wave, base, feat = {}, {}, {}, {}
 
-        def wave_on_vector(s):
-            acc = product("w3", s, "acc_first")[:].rearrange("p b m -> p (b m)")
+        def reduce_on_vector(s, tag):
+            acc = product("w3", s, tag)[:].rearrange("p b m -> p (b m)")
             count = ring.tile([P, S], I32, name="count", tag="turns")
             nc.vector.tensor_scalar(count[:], acc, 1 / (2 * math.pi), None, ALU.mult)
-            rest = ring.tile([P, S], F32, name="rest", tag="reduced")
-            nc.vector.scalar_tensor_tensor(rest[:], count[:], -2 * math.pi, acc, ALU.mult, ALU.add)
-            wave[s] = ring.tile([P, BLOCKS, P], F32, name="wave", tag="wave", bufs=1, align_bytes=64)
-            nc.scalar.activation(wave[s][:].rearrange("p b m -> p (b m)"), rest[:], ACT.Sin)
+            reduced[s] = ring.tile([P, S], F32, name="rest", tag="bend1", bufs=1)
+            nc.vector.scalar_tensor_tensor(reduced[s][:], count[:], -2 * math.pi, acc, ALU.mult, ALU.add)
 
         def wave_front(s, tag="acc_w"):
             acc = product("w3", s, tag)
@@ -223,20 +249,39 @@ def tile_list_slurry_pad_match_kernel(
             nc.vector.scalar_tensor_tensor(reduced[s][:], turns[:].bitcast(I32), -2 * math.pi, folded[:], ALU.mult, ALU.add)
 
         def wave_back(s):
-            wave[s] = ring.tile([P, BLOCKS, P], F32, name="wave", tag="wave", bufs=1, align_bytes=64)
-            nc.scalar.activation(wave[s][:].rearrange("p b m -> p (b m)"), reduced[s][:], ACT.Sin, bias=math.pi / 2)
+            wave[s] = ring.tile([P, BLOCKS, P], F32, name="wave", tag="turn%d" % (s - 1), bufs=1, align_bytes=64)
+            nc.scalar.activation(wave[s][:].rearrange("p b m -> p (b m)"), reduced[s][:], ACT.Sin, bias=0.0 if s == 0 else math.pi / 2)
 
         def make_base(s):
-            acc = product("w1", s, "acc_w")
+            acc = product("w1", s)
             base[s] = ring.tile([P, BLOCKS, P], F32, name="base", tag="base")
             nc.scalar.copy(base[s][:], acc[:])
 
         def make_feat(s):
             b, t = divmod(s, PACK)
-            acc = psum.tile([P, BLOCKS, P], F32, name="acc_sum", tag="acc_sum")
-            add_transposed(acc, [wave[s][:], bend[b][:, :, t, :], base[s][:]] if s == 0 else [base[s][:], bend[b][:, :, t, :], wave[s][:]])
+            acc = psum.tile([P, BLOCKS, P], F32, name="acc_sum", tag="acc_sum%d" % (s % 2), bufs=1)
+            add_transposed(acc, [wave[s][:], bend[b][:, :, t, :], base[s][:]])
             feat[s] = ring.tile([P, S], F32, name="feat", tag="feat")
-            nc.scalar.activation(feat[s][:], acc[:].rearrange("p b m -> p (b m)"), ACT.Copy, scale=gains[:, b, t : t + 1])
+            nc.scalar.activation(feat[s][:], acc[:].rearrange("p b m -> p (b m)"), ACT.Copy, scale=gain_of[s][:])
+
+        def first_feat():
+            acc = psum.tile([P, BLOCKS, P], F32, name="acc_sum", tag="acc_sum0", bufs=1)
+            add_transposed(acc, [wave[0][:], bend[0][:, :, 0, :]])
+            part = ring.tile([P, S], F32, name="part", tag="part", bufs=1, align_bytes=64)
+            nc.scalar.activation(part[:], acc[:].rearrange("p b m -> p (b m)"), ACT.Copy, scale=gain_of[0][:])
+            direct = psum.tile([P, S], F32, name="direct", tag="acc_w", bufs=1)
+            for a in range(PASSES):
+                nc.tensor.matmul_mx(
+                    out=direct[:],
+                    lhsT=w_codes["w1", 0, a, 0][:, :P].bitcast(FP8X4),
+                    lhsT_scale=w_scales["w1", 0, a, 0][:, :P],
+                    rhs=v_codes[a][:].bitcast(FP8X4),
+                    rhs_scale=v_scales[a][:],
+                    start=(a == 0),
+                    stop=(a == PASSES - 1),
+                )
+            feat[0] = ring.tile([P, S], F32, name="feat", tag="feat")
+            nc.vector.scalar_tensor_tensor(feat[0][:], direct[:], gain_of[0][:], part[:], ALU.mult, ALU.add)
 
         slots = {}
         for b in range(HALVES):
@@ -269,44 +314,43 @@ def tile_list_slurry_pad_match_kernel(
             x_codes[side, b] = keep.tile([P, NP], U32, name="c%s%d" % (side, b), align_bytes=64)
             x_scales[side, b] = keep.tile([P, NP], U8, name="s%s%d" % (side, b), align_bytes=64)
 
-        def weave(side, b, half, engine):
+        def weave(side, b, half, engine, tag):
             if half == 0:
-                open_side(side, b, "woven" + side)
+                open_side(side, b, tag)
             cols = slice(half * NP // 2, (half + 1) * NP // 2)
             dst = woven[side, b][:, cols, :].rearrange("p (c i) t -> p c t i", i=4)
             src = slots[side, b][:, :, cols].rearrange("p t (c i) -> p c t i", i=4)
             cast(engine, dst, src)
 
-        def quantise_x(side, b, half):
-            cols = slice(half * NP // 2, (half + 1) * NP // 2)
+        def quantise_x(side, b, cols):
             nc.vector.quantize_mx(
                 out=x_codes[side, b][:, cols].bitcast(FP8X4),
                 scales=x_scales[side, b][:, cols],
                 in_=woven[side, b][:, cols, :].rearrange("p c t -> p (c t)"),
             )
 
-        def weave_and_quantise(side, b, half):
-            weave(side, b, half, "scalar")
-            quantise_x(side, b, half)
+        def weave_and_quantise(side, b, half, tag):
+            weave(side, b, half, "scalar", tag)
+            if half == 1:
+                quantise_x(side, b, slice(0, NP))
 
-        make_bend(0)
-        make_bend(1)
         quantise_weight("w3", 0, 0, 0, "vector")
         quantise_weight("w3", 0, 1, 0, "vector")
-        wave_on_vector(0)
+        reduce_on_vector(0, "acc_sum1")
+        wave_back(0)
+        make_bend(0)
         quantise_weight("w1", 0, 0, 0, "scalar")
-        quantise_weight("w1", 0, 1, 0, "vector", "in_turn", 1)
-        make_base(0)
-        make_feat(0)
+        quantise_weight("w1", 0, 1, 0, "vector")
+        first_feat()
         wave_front(1, "acc_first")
         quantise_weight("w3", 0, 0, 1, "vector")
         quantise_weight("w3", 0, 1, 1, "vector")
-        wave_front(2)
-        quantise_weight("w1", 0, 0, 1, "vector", "in_turn", 1)
-        quantise_weight("w1", 0, 1, 1, "vector", "in_turn", 1)
+        wave_front(2, "acc_sum0")
+        make_bend(1)
 
-        later = [(quantise_weight, name, 1, a, pair, "scalar") for pair in range(2) for name in ("w3", "w1") for a in range(PASSES)]
-        later += [(weave_and_quantise, side, 0, half) for side in ("x1", "x2") for half in range(2)]
+        later = [(round_half, "w1", 0, a, 1, "part", 1) for a in range(PASSES)]
+        later += [(round_half, name, 1, a, pair) for pair in range(2) for name in ("w3", "w1") for a in range(PASSES)]
+        later += [(weave_and_quantise, side, 0, half, tag) for side, tag in (("x1", "turn4"), ("x2", "turn5")) for half in range(2)]
 
         def fill():
             if later:
@@ -316,13 +360,15 @@ def tile_list_slurry_pad_match_kernel(
         for s in range(SLICES):
             put(s)
             fetch(s)
-            if s + 6 < SLICES:
-                load_page(s + 6)
+            if s + 5 < SLICES:
+                load_page(s + 5)
             if s + 1 < SLICES:
                 wave_back(s + 1)
                 make_base(s + 1)
                 fill()
                 make_feat(s + 1)
+                if s < 2:
+                    fill()
             fill()
             if s + 3 < SLICES:
                 wave_front(s + 3)
@@ -330,22 +376,18 @@ def tile_list_slurry_pad_match_kernel(
                 pad_side(s)
 
         last = HALVES - 1
-        open_side("x2", last, "wave")
+        open_side("x2", last, "turn%d" % (SLICES - 1))
         early = PACK - 1
         nc.scalar.copy(woven["x2", last][:, :, :early], slots["x2", last][:, :early, :].rearrange("p t c -> p c t"))
         nc.scalar.activation(
             woven["x2", last][:, :, early], fetched[SLICES - 1][:], ACT.Identity,
             scale=mvecs[:, last, early:], bias=shift_mvec[:],
         )
-        weave("x1", last, 0, "vector")
-        weave("x1", last, 1, "scalar")
-        nc.vector.quantize_mx(
-            out=x_codes["x2", last][:].bitcast(FP8X4),
-            scales=x_scales["x2", last][:],
-            in_=woven["x2", last][:].rearrange("p c t -> p (c t)"),
-        )
-        quantise_x("x1", last, 0)
-        quantise_x("x1", last, 1)
+        weave("x1", last, 0, "vector", "turn0")
+        weave("x1", last, 1, "scalar", "turn0")
+        quantise_x("x2", last, slice(0, NP))
+        quantise_x("x1", last, slice(0, NP // 2))
+        quantise_x("x1", last, slice(NP // 2, NP))
         for mb in range(BLOCKS):
             acc = psum.tile([P, NP], F32, name="acc_e", tag="acc_e", bufs=BLOCKS)
             rows = slice(mb * P, (mb + 1) * P)

import math
from contextlib import ExitStack

import concourse.mybir as mybir
from concourse.masks import make_identity

K, H, T, S, T2, NP = 1024, 1024, 2048, 512, 1024, 512
FLOPS = 2 * 3 * K * H * S + 2 * H * NP * NP

F32 = mybir.dt.float32
BF16 = mybir.dt.bfloat16
I32 = mybir.dt.int32
U32 = mybir.dt.uint32
U16 = mybir.dt.uint16
U8 = mybir.dt.uint8
FP8X4 = mybir.dt.float8_e4m3fn_x4
FP4X4 = mybir.dt.float4_e2m1fn_x4
ACT = mybir.ActivationFunctionType
ALU = mybir.AluOpType

P = 128
PACK = 4
PASS = P * PACK
PASSES = K // PASS
HALVES = H // PASS
SLICES = HALVES * PACK
BLOCKS = S // P
QUADS = 4


def tile_list_slurry_pad_match_kernel(
    tc, tab_words, tab_scales, offs, offs2, offs3, offs4, w1, w2_words, w2_scales, w3, gain, wgs, page0, shift, mvec, pad, out
):
    nc = tc.nc
    with ExitStack() as ctx:
        lists = ctx.enter_context(tc.tile_pool(name="lists", bufs=1))
        keep = ctx.enter_context(tc.tile_pool(name="keep", bufs=1))
        ring = ctx.enter_context(tc.tile_pool(name="ring", bufs=2))
        psum = ctx.enter_context(tc.psum_pool(name="psum", bufs=2))

        def load_list(src, name):
            tile = lists.tile([P, S // 16], U16, name=name)
            nc.sync.dma_start(tile[:], src)
            return tile

        def load_scale_rows(tile, src):
            for q in range(QUADS):
                nc.sync.dma_start(
                    tile[32 * q : 32 * q + 4, :, :].bitcast(I32),
                    src[:, 4 * q : 4 * q + 4, :].rearrange("a r c -> r a c").bitcast(I32),
                )

        def load_row_vector(src, name):
            tile = keep.tile([P, HALVES, PACK], F32, name=name)
            nc.gpsimd.dma_start(tile[:], src.rearrange("(b p t) -> p b t", p=P, t=PACK))
            return tile

        raw = {}

        def load_weight(name, w, b, a):
            tile = ring.tile([P, PACK, PASS], F32, name="raw", tag="raw", bufs=4)
            rows = w[a * PASS : (a + 1) * PASS, b * PASS : (b + 1) * PASS]
            nc.sync.dma_start(tile[:], rows.rearrange("(p i) c -> p i c", i=PACK))
            raw[name, b, a] = tile

        pages = {}

        def load_page(s):
            b, t = divmod(s, PACK)
            tile = ring.tile([P, T2], F32, name="page", tag="page", bufs=5)
            rows = page0[b * PASS : (b + 1) * PASS, :].rearrange("(p t) c -> p t c", t=PACK)
            nc.sync.dma_start(tile[:], rows[:, t, :])
            pages[s] = tile

        tab_scale_rows = keep.tile([P, PASSES, T], U8, name="tab_scale_rows", align_bytes=64)
        nc.vector.memset(tab_scale_rows[:].bitcast(I32), 0)
        w2_scale_rows = keep.tile([P, PASSES, H], U8, name="w2_scale_rows", align_bytes=64)
        nc.vector.memset(w2_scale_rows[:].bitcast(I32), 0)
        ident = keep.tile([P, P], F32, name="ident")
        make_identity(nc, ident[:])
        unread = keep.tile([P, 1], F32, name="unread")
        nc.scalar.activation(unread[:], ident[:, 0:1], ACT.Silu)
        gains = load_row_vector(gain, "gains")
        gain_of = []
        for s in range(SLICES):
            column = ring.tile([P, 1], F32, name="gain_column", tag="turn%d" % s, bufs=1, align_bytes=64)
            nc.gpsimd.tensor_copy(column[:], gains[:, s // PACK, s % PACK : s % PACK + 1])
            gain_of.append(column)
        shifts = load_row_vector(shift, "shifts")
        mvecs = load_row_vector(mvec, "mvecs")

        table = []

        def load_table(a):
            tile = keep.tile([P, T], U32, name="table%d" % a, align_bytes=64)
            nc.sync.dma_start(tile[:].bitcast(I32), tab_words[a].rearrange("p t i -> p (t i)").bitcast(I32))
            table.append(tile)

        wgs_rows = {}

        def load_wgs(first, count):
            tile = keep.tile([P, count, S], F32, name="wgs_rows%d" % first)
            rows = wgs.rearrange("(p t) j -> p t j", t=PACK)[:, first : first + count, :]
            for q in (0, 2, 1, 3):
                nc.sync.dma_start(tile[32 * q : 32 * q + 32, :, :], rows)
            for t in range(count):
                wgs_rows[first + t] = tile[:, t, :]

        pick = load_list(offs, "pick")
        load_table(0)
        place = load_list(offs2, "place")
        pick_pad = load_list(offs4, "pick_pad")
        load_scale_rows(tab_scale_rows, tab_scales)
        load_table(1)
        w2_codes = keep.tile([P, PASSES, 2 * H], U8, name="w2_codes", align_bytes=64)
        nc.sync.dma_start(w2_codes[:].bitcast(I32), w2_words.rearrange("a p c -> p a c").bitcast(I32))
        load_scale_rows(w2_scale_rows, w2_scales)
        load_weight("w3", w3, 0, 0)
        load_weight("w3", w3, 0, 1)
        load_weight("w1", w1, 0, 0)
        load_weight("w1", w1, 0, 1)
        load_wgs(0, 1)
        load_page(0)
        pick_slurry = load_list(offs3, "pick_slurry")
        load_wgs(1, PACK - 1)
        load_page(1)
        load_weight("w3", w3, 1, 0)
        load_weight("w3", w3, 1, 1)
        load_weight("w1", w1, 1, 0)
        load_weight("w1", w1, 1, 1)
        for s in range(2, 5):
            load_page(s)
        pad_rows = keep.tile([P, NP], F32, name="pad_rows")
        nc.sync.dma_start(pad_rows[:], pad.partition_broadcast(P))

        v_codes, v_scales = [], []
        for a in range(PASSES):
            scales = keep.tile([P, S], U8, name="v_scales%d" % a, align_bytes=64)
            nc.vector.tensor_copy(scales[:], tab_scale_rows[:, a, :].indirect(pick[:]))
            codes = keep.tile([P, S], U32, name="v_codes%d" % a, align_bytes=64)
            nc.vector.tensor_copy(codes[:], table[a][:].indirect(pick[:]))
            v_codes.append(codes)
            v_scales.append(scales)

        w_codes, w_scales = {}, {}

        def cast(engine, dst, src):
            if engine == "vector":
                nc.vector.tensor_copy(dst, src)
            elif engine == "scalar":
                nc.scalar.copy(dst, src)
            else:
                nc.gpsimd.tensor_scalar(dst, src, 1.0, 0.0, ALU.mult, ALU.add)

        def quantise_weight(name, b, a, pair, engine):
            grouped = ring.tile([P, 2, P, PACK], BF16, name="grouped", tag="grouped", bufs=3, align_bytes=64)
            src = raw[name, b, a][:].rearrange("p i (m t) -> p m i t", t=PACK)[:, :, :, 2 * pair : 2 * pair + 2]
            cast(engine, grouped[:].rearrange("p t m i -> p m i t"), src)
            label = "%s_%d%d%d" % (name, b, a, pair)
            codes = keep.tile([P, 2 * P], U32, name="c" + label, align_bytes=64)
            scales = keep.tile([P, 2 * P], U8, name="s" + label, align_bytes=64)
            nc.vector.quantize_mx(out=codes[:].bitcast(FP8X4), scales=scales[:], in_=grouped[:].rearrange("p t m i -> p (t m i)"))
            w_codes[name, b, a, pair] = codes
            w_scales[name, b, a, pair] = scales

        both = {}

        def round_half(name, b, a, pair, tag="both", bufs=2):
            if a == 0:
                both[name, b, pair] = ring.tile([P, PASSES, 2, P, PACK], BF16, name="both", tag=tag, bufs=bufs, align_bytes=64)
            grouped = both[name, b, pair]
            src = raw[name, b, a][:].rearrange("p i (m t) -> p m i t", t=PACK)[:, :, :, 2 * pair : 2 * pair + 2]
            nc.scalar.copy(grouped[:, a].rearrange("p t m i -> p m i t"), src)
            if a == PASSES - 1:
                label = "%s_%d%d" % (name, b, pair)
                codes = keep.tile([P, PASSES, 2 * P], U32, name="c" + label, align_bytes=64)
                scales = keep.tile([P, PASSES, 2 * P], U8, name="s" + label, align_bytes=64)
                nc.vector.quantize_mx(
                    out=codes[:].rearrange("p a c -> p (a c)").bitcast(FP8X4),
                    scales=scales[:].rearrange("p a c -> p (a c)"),
                    in_=grouped[:].rearrange("p a t m i -> p (a t m i)"),
                )
                for n in range(PASSES):
                    w_codes[name, b, n, pair] = codes[:, n, :]
                    w_scales[name, b, n, pair] = scales[:, n, :]

        def product(name, s, tag="acc_w"):
            b, t = divmod(s, PACK)
            pair, cols = t // 2, slice((t % 2) * P, (t % 2 + 1) * P)
            acc = psum.tile([P, BLOCKS, P], F32, name=tag, tag=tag, bufs=1)
            for jb in range(BLOCKS):
                picked = slice(jb * P, (jb + 1) * P)
                for a in range(PASSES):
                    nc.tensor.matmul_mx(
                        out=acc[:, jb, :],
                        lhsT=v_codes[a][:, picked].bitcast(FP8X4),
                        lhsT_scale=v_scales[a][:, picked],
                        rhs=w_codes[name, b, a, pair][:, cols].bitcast(FP8X4),
                        rhs_scale=w_scales[name, b, a, pair][:, cols],
                        start=(a == 0),
                        stop=(a == PASSES - 1),
                    )
            return acc

        def add_transposed(acc, terms):
            for n, term in enumerate(terms):
                for jb in range(BLOCKS):
                    nc.tensor.matmul(
                        acc[:, jb, :], term[:, jb, :], ident[:], is_transpose=True,
                        start=(n == 0 and jb == 0), stop=(n == len(terms) - 1 and jb == BLOCKS - 1),
                    )

        bend = {}

        def make_bend(b):
            tile = ring.tile([P, BLOCKS, PACK, P], F32, name="bend", tag="bend%d" % b, bufs=1)
            for jb in range(BLOCKS):
                picked = slice(jb * P, (jb + 1) * P)
                acc = psum.tile([P, PASS], F32, name="acc_bend", tag="acc_e", bufs=BLOCKS)
                for a in range(PASSES):
                    nc.tensor.matmul_mx(
                        out=acc[:],
                        lhsT=v_codes[a][:, picked].bitcast(FP8X4),
                        lhsT_scale=v_scales[a][:, picked],
                        rhs=w2_codes[:, a, 2 * b * PASS : 2 * (b + 1) * PASS].bitcast(FP4X4),
                        rhs_scale=w2_scale_rows[:, a, b * PASS : (b + 1) * PASS],
                        start=(a == 0),
                        stop=(a == PASSES - 1),
                    )
                nc.scalar.activation(tile[:, jb, :, :], acc[:].rearrange("p (m t) -> p t m", t=PACK), ACT.Tanh)
            bend[b] = tile

        reduced, wave, base, feat = {}, {}, {}, {}

        def reduce_on_vector(s, tag):
            acc = product("w3", s, tag)[:].rearrange("p b m -> p (b m)")
            count = ring.tile([P, S], I32, name="count", tag="turns")
            nc.vector.tensor_scalar(count[:], acc, 1 / (2 * math.pi), None, ALU.mult)
            reduced[s] = ring.tile([P, S], F32, name="rest", tag="bend1", bufs=1)
            nc.vector.scalar_tensor_tensor(reduced[s][:], count[:], -2 * math.pi, acc, ALU.mult, ALU.add)

        def wave_front(s, tag="acc_w"):
            acc = product("w3", s, tag)
            folded = ring.tile([P, S], F32, name="folded", tag="folded")
            nc.scalar.activation(folded[:], acc[:].rearrange("p b m -> p (b m)"), ACT.Abs, bias=-math.pi / 2)
            turns = ring.tile([P, S], U32, name="turns", tag="turns")
            nc.scalar.activation(turns[:], folded[:], ACT.Copy, scale=1 / (2 * math.pi), bias=0.25)
            reduced[s] = ring.tile([P, S], F32, name="reduced", tag="reduced")
            nc.vector.scalar_tensor_tensor(reduced[s][:], turns[:].bitcast(I32), -2 * math.pi, folded[:], ALU.mult, ALU.add)

        def wave_back(s):
            wave[s] = ring.tile([P, BLOCKS, P], F32, name="wave", tag="turn%d" % (s - 1), bufs=1, align_bytes=64)
            nc.scalar.activation(wave[s][:].rearrange("p b m -> p (b m)"), reduced[s][:], ACT.Sin, bias=0.0 if s == 0 else math.pi / 2)

        def make_base(s):
            acc = product("w1", s)
            base[s] = ring.tile([P, BLOCKS, P], F32, name="base", tag="base")
            nc.scalar.copy(base[s][:], acc[:])

        def make_feat(s):
            b, t = divmod(s, PACK)
            acc = psum.tile([P, BLOCKS, P], F32, name="acc_sum", tag="acc_sum%d" % (s % 2), bufs=1)
            add_transposed(acc, [wave[s][:], bend[b][:, :, t, :], base[s][:]])
            feat[s] = ring.tile([P, S], F32, name="feat", tag="feat")
            nc.scalar.activation(feat[s][:], acc[:].rearrange("p b m -> p (b m)"), ACT.Copy, scale=gain_of[s][:])

        def first_feat():
            acc = psum.tile([P, BLOCKS, P], F32, name="acc_sum", tag="acc_sum0", bufs=1)
            add_transposed(acc, [wave[0][:], bend[0][:, :, 0, :]])
            part = ring.tile([P, S], F32, name="part", tag="part", bufs=1, align_bytes=64)
            nc.scalar.activation(part[:], acc[:].rearrange("p b m -> p (b m)"), ACT.Copy, scale=gain_of[0][:])
            direct = psum.tile([P, S], F32, name="direct", tag="acc_w", bufs=1)
            for a in range(PASSES):
                nc.tensor.matmul_mx(
                    out=direct[:],
                    lhsT=w_codes["w1", 0, a, 0][:, :P].bitcast(FP8X4),
                    lhsT_scale=w_scales["w1", 0, a, 0][:, :P],
                    rhs=v_codes[a][:].bitcast(FP8X4),
                    rhs_scale=v_scales[a][:],
                    start=(a == 0),
                    stop=(a == PASSES - 1),
                )
            feat[0] = ring.tile([P, S], F32, name="feat", tag="feat")
            nc.vector.scalar_tensor_tensor(feat[0][:], direct[:], gain_of[0][:], part[:], ALU.mult, ALU.add)

        slots = {}
        for b in range(HALVES):
            for side in ("x1", "x2"):
                slots[side, b] = keep.tile([P, PACK, NP], BF16, name="slots_%s%d" % (side, b))
        fetched = {}

        def put(s):
            nc.vector.tensor_tensor(pages[s][:].indirect(place[:]), feat[s][:], wgs_rows[s % PACK], ALU.mult)

        def fetch(s):
            b, t = divmod(s, PACK)
            fetched[s] = ring.tile([P, NP], F32, name="fetched", tag="fetched")
            nc.vector.tensor_copy(fetched[s][:], pages[s][:].indirect(pick_pad[:]))
            nc.vector.tensor_copy(slots["x1", b][:, t, :], pages[s][:].indirect(pick_slurry[:]))

        shift_mvec = keep.tile([P, 1], F32, name="shift_mvec")
        nc.gpsimd.tensor_tensor(shift_mvec[:], shifts[:, HALVES - 1, PACK - 1 :], mvecs[:, HALVES - 1, PACK - 1 :], ALU.mult)

        def pad_side(s):
            b, t = divmod(s, PACK)
            nc.gpsimd.tensor_scalar(
                slots["x2", b][:, t, :], fetched[s][:], shifts[:, b, t : t + 1], mvecs[:, b, t : t + 1], ALU.add, ALU.mult
            )

        woven, x_codes, x_scales = {}, {}, {}

        def open_side(side, b, tag):
            woven[side, b] = ring.tile([P, NP, PACK], BF16, name="woven", tag=tag, bufs=1, align_bytes=64)
            x_codes[side, b] = keep.tile([P, NP], U32, name="c%s%d" % (side, b), align_bytes=64)
            x_scales[side, b] = keep.tile([P, NP], U8, name="s%s%d" % (side, b), align_bytes=64)

        def weave(side, b, half, engine, tag):
            if half == 0:
                open_side(side, b, tag)
            cols = slice(half * NP // 2, (half + 1) * NP // 2)
            dst = woven[side, b][:, cols, :].rearrange("p (c i) t -> p c t i", i=4)
            src = slots[side, b][:, :, cols].rearrange("p t (c i) -> p c t i", i=4)
            cast(engine, dst, src)

        def quantise_x(side, b, cols):
            nc.vector.quantize_mx(
                out=x_codes[side, b][:, cols].bitcast(FP8X4),
                scales=x_scales[side, b][:, cols],
                in_=woven[side, b][:, cols, :].rearrange("p c t -> p (c t)"),
            )

        def weave_and_quantise(side, b, half, tag):
            weave(side, b, half, "scalar", tag)
            if half == 1:
                quantise_x(side, b, slice(0, NP))

        quantise_weight("w3", 0, 0, 0, "vector")
        quantise_weight("w3", 0, 1, 0, "vector")
        reduce_on_vector(0, "acc_sum1")
        wave_back(0)
        make_bend(0)
        quantise_weight("w1", 0, 0, 0, "scalar")
        quantise_weight("w1", 0, 1, 0, "vector")
        first_feat()
        wave_front(1, "acc_first")
        quantise_weight("w3", 0, 0, 1, "vector")
        quantise_weight("w3", 0, 1, 1, "vector")
        wave_front(2, "acc_sum0")
        make_bend(1)

        later = [(round_half, "w1", 0, a, 1, "part", 1) for a in range(PASSES)]
        later += [(round_half, name, 1, a, pair) for pair in range(2) for name in ("w3", "w1") for a in range(PASSES)]
        later += [(weave_and_quantise, side, 0, half, tag) for side, tag in (("x1", "turn4"), ("x2", "turn5")) for half in range(2)]

        def fill():
            if later:
                step = later.pop(0)
                step[0](*step[1:])

        for s in range(SLICES):
            put(s)
            fetch(s)
            if s + 5 < SLICES:
                load_page(s + 5)
            if s + 1 < SLICES:
                wave_back(s + 1)
                make_base(s + 1)
                fill()
                make_feat(s + 1)
                if s < 2:
                    fill()
            fill()
            if s + 3 < SLICES:
                wave_front(s + 3)
            if s + 1 < SLICES:
                pad_side(s)

        last = HALVES - 1
        open_side("x2", last, "turn%d" % (SLICES - 1))
        early = PACK - 1
        nc.scalar.copy(woven["x2", last][:, :, :early], slots["x2", last][:, :early, :].rearrange("p t c -> p c t"))
        nc.scalar.activation(
            woven["x2", last][:, :, early], fetched[SLICES - 1][:], ACT.Identity,
            scale=mvecs[:, last, early:], bias=shift_mvec[:],
        )
        weave("x1", last, 0, "vector", "turn0")
        weave("x1", last, 1, "scalar", "turn0")
        quantise_x("x2", last, slice(0, NP))
        quantise_x("x1", last, slice(0, NP // 2))
        quantise_x("x1", last, slice(NP // 2, NP))
        for mb in range(BLOCKS):
            acc = psum.tile([P, NP], F32, name="acc_e", tag="acc_e", bufs=BLOCKS)
            rows = slice(mb * P, (mb + 1) * P)
            for b in reversed(range(HALVES)):
                nc.tensor.matmul_mx(
                    out=acc[:],
                    lhsT=x_codes["x1", b][:, rows].bitcast(FP8X4),
                    lhsT_scale=x_scales["x1", b][:, rows],
                    rhs=x_codes["x2", b][:].bitcast(FP8X4),
                    rhs_scale=x_scales["x2", b][:],
                    start=(b == last),
                    stop=(b == 0),
                )
            result = keep.tile([P, NP], F32, name="result%d" % mb)
            nc.vector.tensor_tensor(result[:], acc[:], pad_rows[:], ALU.mult)
            nc.sync.dma_start(out[mb * P : (mb + 1) * P, :], result[:])
